import numpy as np
import ml_dtypes


def mxq(x, axis, fmt="e4m3"):
    dtype, down = {"e4m3": (ml_dtypes.float8_e4m3fn, 7), "e5m2": (ml_dtypes.float8_e5m2, 14)}[fmt]
    v = np.moveaxis(np.asarray(x, np.float32).astype(ml_dtypes.bfloat16).astype(np.float64), axis, -1)
    blocks = v.reshape(v.shape[:-1] + (-1, 32))
    amax = np.abs(blocks).max(-1, keepdims=True)
    byte = np.maximum(np.where(amax > 0, np.frexp(amax)[1] - 1 + 127, 0) - down, 1)
    scale = np.exp2(byte - 127.0)
    codes = (blocks / scale).astype(np.float32).astype(dtype).astype(np.float64)
    return np.moveaxis((codes * scale).reshape(v.shape), -1, axis)


WIDE = False


def mx_kscale(k):
    if not WIDE:
        return np.ones(k)
    levels = np.array([10, -10, 5, -5, 0])
    if k % 512:
        return np.exp2(np.random.permutation(np.resize(levels, k // 32))).repeat(32)
    a = np.empty((k // 512, 16))
    for p in range(k // 512):
        a[p, :8] = np.random.permutation(np.resize(levels, 8))
        for g in range(8):
            far = levels[np.abs(levels - a[p, g]) >= 10]
            a[p, g + 8] = far[np.random.randint(len(far))]
    return np.exp2(a.ravel()).repeat(32)


BF16 = ml_dtypes.bfloat16


def bf(x):
    return np.asarray(x, np.float32).astype(BF16)


def f64(x):
    return np.asarray(x).astype(np.float64)


T, K, F, Q = 2048, 1024, 512, 1024


def setup_inputs():
    s, t = mx_kscale(K), mx_kscale(T)
    loudness = np.exp(0.7 * np.random.standard_normal((T, 1)))
    return {"power": bf(np.exp(np.random.standard_normal((T, K)) - 0.5) * loudness * s),
            "filters": bf(np.exp(2.0 * np.random.standard_normal((K, F)) - 2.0) / K / s[:, None]),
            "offset": bf(0.1 + 0.4 * np.random.random(F)),
            "gain": bf(1.0 + 0.1 * np.random.standard_normal(F)),
            "bias": bf(0.3 * np.random.standard_normal(F)),
            "frame_weight": bf((0.5 + 0.5 * np.random.random(T)) * t),
            "basis": bf(np.random.standard_normal((Q, T)) / np.sqrt(T) / t),
            "lifter": bf(1.0 + 0.1 * np.random.standard_normal(Q))}


def reference(power, filters, offset, gain, bias, frame_weight, basis, lifter):
    e = mxq(f64(power), 1, "e4m3") @ mxq(f64(filters), 0, "e4m3")
    y = f64(gain) * np.log(e + f64(offset)) + f64(bias)
    h = f64(frame_weight)[:, None] * y
    c = mxq(f64(basis), 1, "e4m3") @ mxq(h, 0, "e4m3")
    return f64(lifter)[:, None] * c

@@ -1,0 +1,321 @@
+from contextlib import ExitStack
+
+import concourse.mybir as mybir
+from concourse.masks import make_identity
+
+T, K, F, Q = 2048, 1024, 512, 1024
+FLOPS = 2 * T * K * F + 2 * Q * T * F
+
+F32 = mybir.dt.float32
+BF16 = mybir.dt.bfloat16
+U32 = mybir.dt.uint32
+U8 = mybir.dt.uint8
+FP8X4 = mybir.dt.float8_e4m3fn_x4
+ACT = mybir.ActivationFunctionType
+ALU = mybir.AluOpType
+
+P = 128
+PACK = 4
+PASS = P * PACK
+BANK = 512
+GROUPS = T // PASS
+BIN_PASSES = K // PASS
+CHUNKS = F // P
+QTILES = Q // P
+BANKS = 8
+LAG_TURN = 4
+SORTED = [5, 7, 9, 11, 12, 13, 14, 15]
+AFFINE_ON = "vvvvvvvvvvvvvvvv"
+SORT_AHEAD = 2
+TAIL = 256
+QH_LATE = False
+LIFT_ON = "vsvsvsvs"
+
+
+def tile_temporal_log_mel_cepstrum_f4_kernel(
+    tc, power, filters, offset, gain, bias, frame_weight, basis, lifter, out
+):
+    nc = tc.nc
+    with ExitStack() as ctx:
+        keep = ctx.enter_context(tc.tile_pool(name="keep", bufs=1))
+        ring = ctx.enter_context(tc.tile_pool(name="ring", bufs=3))
+        psum = ctx.enter_context(tc.psum_pool(name="psum", bufs=1))
+        ctx.enter_context(tc.manual_schedule())
+
+        idle_banks = ["bank%d" % n for n in range(BANKS)]
+        held = {}
+
+        def take_bank(use):
+            tag = idle_banks[0]
+            idle_banks.remove(tag)
+            held[use] = (tag, psum.tile([P, BANK], F32, name=tag, tag=tag))
+            return held[use][1]
+
+        def last_read(use):
+            tag, bank = held[use]
+            idle_banks.append(tag)
+            return bank
+
+        ident = keep.tile([P, P], F32, name="ident")
+        rows16 = keep.tile([P, P], BF16, name="rows16")
+        rows32 = keep.tile([P, P], F32, name="rows32")
+        cols = keep.tile([P, 32], F32, name="cols")
+        one = keep.tile([P, 1], F32, name="one")
+        warm = keep.tile([P, 1], F32, name="warm")
+        weight = keep.tile([P, GROUPS, PACK], BF16, name="weight")
+
+        raw = [keep.tile([P, PACK, PASS], BF16, name="raw%d" % a) for a in range(16)]
+        codes = [keep.tile([P, PASS], U32, name="codes%d" % a, align_bytes=64) for a in range(16)]
+        scales = [keep.tile([P, PASS], U8, name="scales%d" % a, align_bytes=64) for a in range(16)]
+        filt_raw = [keep.tile([P, PACK, F], BF16, name="filt_raw%d" % c) for c in range(BIN_PASSES)]
+        filt_16 = [keep.tile([P, F, PACK], BF16, name="filt_16_%d" % c, align_bytes=64) for c in range(BIN_PASSES)]
+        filt_codes = [keep.tile([P, F], U32, name="filt_codes%d" % c, align_bytes=64) for c in range(BIN_PASSES)]
+        filt_scales = [keep.tile([P, F], U8, name="filt_scales%d" % c, align_bytes=64) for c in range(BIN_PASSES)]
+        h16 = [keep.tile([P, F, PACK], BF16, name="h16_%d" % g, align_bytes=64) for g in range(GROUPS)]
+        h_codes = [keep.tile([P, F], U32, name="h_codes%d" % g, align_bytes=64) for g in range(GROUPS)]
+        h_scales = [keep.tile([P, F], U8, name="h_scales%d" % g, align_bytes=64) for g in range(GROUPS)]
+
+        def load_operand(a):
+            if a < 8:
+                g, c = divmod(a, BIN_PASSES)
+                src = power[g * PASS : (g + 1) * PASS, c * PASS : (c + 1) * PASS].rearrange("(m t) k -> m t k", t=PACK)
+            else:
+                i = a - 8
+                src = basis[i * P : (i + 1) * P, :].rearrange("q (g k) -> q g k", g=GROUPS)
+            nc.sync.dma_start(out=raw[a][:], in_=src)
+
+        def load_filters(c):
+            src = filters[c * PASS : (c + 1) * PASS, :]
+            nc.sync.dma_start(out=filt_raw[c][:], in_=src.rearrange("(p j) f -> p j f", j=PACK))
+
+        make_identity(nc, ident[:])
+        nc.vector.memset(rows16[:], 0.0)
+        nc.vector.memset(one[:], 1.0)
+        load_operand(0)
+        load_filters(0)
+        nc.scalar.dma_start(out=rows16[0:4, :], in_=offset.rearrange("(j p) -> j p", p=P))
+        nc.scalar.dma_start(out=rows16[4:8, :], in_=gain.rearrange("(j p) -> j p", p=P))
+        nc.scalar.dma_start(out=rows16[8:12, :], in_=bias.rearrange("(j p) -> j p", p=P))
+        nc.scalar.dma_start(out=rows16[16:24, :], in_=lifter.rearrange("(i p) -> i p", p=P))
+        nc.scalar.activation(out=warm[:], in_=one[:], func=ACT.Ln)
+        load_operand(1)
+        load_operand(2)
+        load_filters(1)
+        load_operand(3)
+        nc.sync.dma_start(out=weight[:], in_=frame_weight.rearrange("(g m t) -> m g t", m=P, t=PACK))
+        for a in range(4, 16):
+            load_operand(a)
+
+        words = {}
+        grouped = {}
+
+        def sort_words(a):
+            tile = ring.tile([P, PACK, 2, P], F32, name="sorted", tag="sorted", bufs=4)
+            src = raw[a][:].rearrange("p s k -> p (s k)").bitcast(F32)
+            nc.vector.tensor_copy(out=tile[:], in_=src.rearrange("p (s w u) -> p s u w", s=PACK, u=2))
+            words[a] = tile
+
+        def turn_operand(a, half):
+            bank = take_bank(("operand", a, half))
+            view = bank[:].rearrange("p (s u m) -> p s u m", s=2, u=2)
+            src = raw[a][:].rearrange("p s k -> p (s k)").bitcast(F32)
+            for s in range(2):
+                slot = 2 * half + s
+                for u in range(2):
+                    if a in words:
+                        piece = words[a][:, slot, u, :]
+                    else:
+                        piece = src[:, 256 * slot + u : 256 * (slot + 1) : 2]
+                    nc.tensor.transpose(view[:, s, u, :], piece, ident[:])
+
+        def gather_operand(a, half):
+            if half == 0:
+                grouped[a] = ring.tile([P, PACK * P * PACK], BF16, name="grouped", tag="grouped", align_bytes=64)
+            dst = grouped[a][:, 1024 * half : 1024 * (half + 1)].bitcast(F32)
+            nc.scalar.copy(
+                out=dst.rearrange("p (s m u) -> p s m u", s=2, u=2),
+                in_=last_read(("operand", a, half))[:].rearrange("p (s u m) -> p s m u", s=2, u=2),
+            )
+
+        def quantize_operand(a):
+            nc.vector.quantize_mx(out=codes[a][:].bitcast(FP8X4), scales=scales[a][:], in_=grouped[a][:])
+
+        def interleave_filters(c, h):
+            span = slice(256 * h, 256 * (h + 1))
+            nc.vector.tensor_copy(
+                out=filt_16[c][:, span, :].rearrange("p (n i) j -> p n j i", i=4),
+                in_=filt_raw[c][:, :, span].rearrange("p j (n i) -> p n j i", i=4),
+            )
+
+        def quantize_filters(c, h):
+            span = slice(256 * h, 256 * (h + 1))
+            nc.vector.quantize_mx(
+                out=filt_codes[c][:, span].bitcast(FP8X4),
+                scales=filt_scales[c][:, span],
+                in_=filt_16[c][:, span, :].rearrange("p f j -> p (f j)"),
+            )
+
+        logs = {}
+        levels = {}
+
+        def mel_matmul(g, j, passes):
+            if passes[0] == 0:
+                take_bank(("energy", g, j))
+            bank = held["energy", g, j][1]
+            for c in passes:
+                a = BIN_PASSES * g + c
+                nc.tensor.matmul_mx(
+                    out=bank[:],
+                    lhsT=filt_codes[c][:, j * P : (j + 1) * P].bitcast(FP8X4),
+                    lhsT_scale=filt_scales[c][:, j * P : (j + 1) * P],
+                    rhs=codes[a][:].bitcast(FP8X4),
+                    rhs_scale=scales[a][:],
+                    start=(c == 0),
+                    stop=(c == BIN_PASSES - 1),
+                )
+
+        def take_log(g, j):
+            logs[g, j] = ring.tile([P, PASS], F32, name="logs", tag="logs")
+            nc.scalar.activation(out=logs[g, j][:], in_=last_read(("energy", g, j))[:], func=ACT.Ln, bias=cols[:, j : j + 1])
+
+        def gain_and_bias(g, j):
+            levels[g, j] = ring.tile([P, PASS], F32, name="levels", tag="levels", bufs=6)
+            where = AFFINE_ON[4 * g + j]
+            if where == "s":
+                nc.scalar.activation(
+                    out=levels[g, j][:],
+                    in_=logs[g, j][:],
+                    func=ACT.Identity,
+                    scale=cols[:, 4 + j : 5 + j],
+                    bias=cols[:, 8 + j : 9 + j],
+                )
+            else:
+                engine = nc.vector if where == "v" else nc.gpsimd
+                engine.tensor_scalar(
+                    out=levels[g, j][:],
+                    in0=logs[g, j][:],
+                    scalar1=cols[:, 4 + j : 5 + j],
+                    scalar2=cols[:, 8 + j : 9 + j],
+                    op0=ALU.mult,
+                    op1=ALU.add,
+                )
+
+        def turn_levels(g, j):
+            bank = take_bank(("levels", g, j))
+            for t in range(PACK):
+                nc.tensor.transpose(bank[:, t * P : (t + 1) * P], levels[g, j][:, t * P : (t + 1) * P], ident[:])
+
+        def weigh_frames(g, j):
+            nc.vector.tensor_tensor(
+                out=h16[g][:, j * P : (j + 1) * P, :],
+                in0=last_read(("levels", g, j))[:].rearrange("p (t f) -> p f t", t=PACK),
+                in1=weight[:, g, :].unsqueeze(1).broadcast_to([P, P, PACK]),
+                op=ALU.mult,
+            )
+
+        def quantize_h(g):
+            nc.vector.quantize_mx(
+                out=h_codes[g][:].bitcast(FP8X4), scales=h_scales[g][:], in_=h16[g][:].rearrange("p f t -> p (f t)")
+            )
+
+        def cepstrum_matmul(i, span, groups):
+            if groups[0] == 0:
+                take_bank(("sums", i, span.start))
+            bank = held["sums", i, span.start][1]
+            for g in groups:
+                nc.tensor.matmul_mx(
+                    out=bank[:, 0 : span.stop - span.start],
+                    lhsT=codes[8 + i][:, g * P : (g + 1) * P].bitcast(FP8X4),
+                    lhsT_scale=scales[8 + i][:, g * P : (g + 1) * P],
+                    rhs=h_codes[g][:, span].bitcast(FP8X4),
+                    rhs_scale=h_scales[g][:, span],
+                    start=(g == 0),
+                    stop=(g == GROUPS - 1),
+                )
+
+        def lift_and_store(i, span, where):
+            width = span.stop - span.start
+            bank = last_read(("sums", i, span.start))[:, 0:width]
+            result = ring.tile([P, width], F32, name="result", tag="result", bufs=4)
+            if where == "v":
+                nc.vector.tensor_scalar(
+                    out=result[:], in0=bank, scalar1=cols[:, 16 + i : 17 + i], scalar2=None, op0=ALU.mult
+                )
+            else:
+                nc.scalar.activation(out=result[:], in_=bank, func=ACT.Copy, scale=cols[:, 16 + i : 17 + i])
+            nc.sync.dma_start(out=out[i * P : (i + 1) * P, span], in_=result[:])
+
+        def pair(n):
+            g, h = divmod(n, 2)
+            return [(g, 2 * h), (g, 2 * h + 1)] if 0 <= n < 2 * GROUPS else []
+
+        whole = slice(0, F)
+        every = list(range(GROUPS))
+        second = {
+            10: [(0, whole, [0, 1, 2])],
+            11: [(1, whole, [0, 1, 2])],
+            12: [(2, whole, [0, 1, 2]), (0, whole, [3]), (1, whole, [3]), (2, whole, [3])],
+        }
+        for i in range(3, QTILES - 1):
+            second[10 + i] = [(i, whole, every)]
+        second[17] = [(7, slice(w, w + TAIL), every) for w in range(0, F, TAIL)]
+        finished = []
+
+        for step in range(19):
+            a = step
+            turning = pair(step - LAG_TURN)
+            logging = pair(step - 3)
+            for g, j in logging:
+                take_log(g, j)
+            for g, j in turning:
+                turn_levels(g, j)
+            if step == 1:
+                interleave_filters(0, 0)
+                nc.vector.tensor_copy(out=rows32[:], in_=rows16[:])
+                quantize_filters(0, 0)
+            if a < 16:
+                turn_operand(a, 0)
+                turn_operand(a, 1)
+            if step == 1:
+                bank = take_bank("vectors")
+                nc.tensor.transpose(bank[:, 0:P], rows32[:], ident[:])
+            if 1 <= a <= 16:
+                quantize_operand(a - 1)
+            if step == 1:
+                interleave_filters(0, 1)
+                nc.vector.tensor_copy(out=cols[:], in_=last_read("vectors")[:, 0:32])
+                quantize_filters(0, 1)
+            if step == 2:
+                interleave_filters(1, 0)
+                quantize_filters(1, 0)
+                interleave_filters(1, 1)
+            if step == 3:
+                quantize_filters(1, 1)
+            done_pair = step - LAG_TURN - 1
+            if QH_LATE and done_pair % 2 == 1 and 0 <= done_pair < 2 * GROUPS:
+                quantize_h(done_pair // 2)
+            for n, (i, span) in enumerate(finished):
+                lift_and_store(i, span, LIFT_ON[i] if i < 7 else "sv"[n % 2])
+            finished = []
+            for n in range(2):
+                if turning:
+                    weigh_frames(*turning[n])
+                if logging:
+                    gain_and_bias(*logging[n])
+            if a + SORT_AHEAD in SORTED:
+                sort_words(a + SORT_AHEAD)
+            done_pair = step - LAG_TURN
+            if not QH_LATE and done_pair % 2 == 1 and 0 <= done_pair < 2 * GROUPS:
+                quantize_h(done_pair // 2)
+            if a < 16:
+                gather_operand(a, 0)
+                gather_operand(a, 1)
+            if step in (1, 2):
+                for g, j in pair(step - 1):
+                    mel_matmul(g, j, [0])
+            for g, j in pair(step - 2):
+                mel_matmul(g, j, [1] if step in (2, 3) else [0, 1])
+            for i, span, groups in second.get(step, []):
+                cepstrum_matmul(i, span, groups)
+                if groups[-1] == GROUPS - 1:
+                    finished.append((i, span))

@@ -23,13 +23,7 @@ BIN_PASSES = K // PASS
 CHUNKS = F // P
 QTILES = Q // P
 BANKS = 8
-LAG_TURN = 4
-SORTED = [5, 7, 9, 11, 12, 13, 14, 15]
-AFFINE_ON = "vvvvvvvvvvvvvvvv"
-SORT_AHEAD = 2
-TAIL = 256
-QH_LATE = False
-LIFT_ON = "vsvsvsvs"
+ORDER = "t0_1:P c0_1:S i0_1:S cast:V t0_0:P i0_0:V t1_0:P t1_1:P c0_0:V t2_0:P tv:P f0_0:V c1_0:S f0_1:V t2_1:P c1_1:S q0:V i1_0:V c2_0:S q1:V i1_1:S m0_0_0:P f1_0:V m0_2_0:P f1_1:V cols:S t3_1:P t3_0:P m0_1_0:P c2_1:V c3_1:S s4:V c3_0:S m0_2_1:P s5:V l0_2:S m0_0_1:P m0_1_1:P l0_1:S q2:V m0_3_0:P m0_3_1:P t4_0:P t5_1:P a0_2:V t5_0:P l0_3:S t4_1:P c4_0:S c5_0:S s6:V c5_1:S u0_2:P q3:V t6_0:P a0_1:V h0_2:V c4_1:S q4:V a0_3:V s8:V t7_0:P c6_0:S q5:V m1_1_0:P m1_2_0:P m1_3_0:P c7_0:S m1_1_1:P m1_0_0:P m1_3_1:P m1_0_1:P l1_1:S m1_2_1:P l1_3:S t6_1:P t7_1:P l1_0:S c7_1:S t9_0:P u0_1:P l1_2:S a1_1:V c6_1:V a1_3:V t8_0:P t9_1:P u0_3:P c9_0:S a1_0:V u1_3:P h0_1:V u1_0:P q7:V l0_0:S a1_2:V c9_1:S t8_1:P q6:V m2_0_0:P h1_3:V c8_0:S m2_1_0:P m2_1_1:P c8_1:S m3_0_0:P l2_1:S m3_2_0:P m2_2_0:P m2_0_1:P m3_2_1:P a0_0:S m3_0_1:P s11:V h1_0:V l2_0:S m2_2_1:P q9:V m2_3_0:P m3_3_0:P m3_1_0:P a2_1:V m3_1_1:P m3_3_1:P l3_0:S u1_1:P u1_2:P l2_2:S l3_2:S h0_3:V m2_3_1:P s15:V t11_0:P q8:V a2_2:V a2_0:V a3_0:S h1_1:V u0_0:P l2_3:S h1_2:V u2_0:P l3_3:S t12_1:P c11_0:S a3_2:V t11_1:P h2_0:V h0_0:V c11_1:S l3_1:S u3_0:P a2_3:S u3_2:P h3_0:V h3_2:V u2_1:P q11:V t14_1:P t12_0:P t14_0:P u2_2:P c14_1:S c12_0:S t15_0:P t10_0:P a3_3:S t10_1:P h2_1:V h2_2:V H0:V c15_0:S u2_3:P u3_3:P h2_3:V a3_1:S t15_1:P t13_1:P c14_0:S h3_3:V c12_1:S H1:V u3_1:P c10_0:S q14:V h3_1:V t13_0:P x3_0_0:P x3_0_1:P x1_0_0:P H2:V x6_0_0:P x6_0_1:P x1_0_1:P c10_1:S x0_0_0:P H3:V x0_0_1:P x0_0_2:P c13_0:S x6_0_2:P x0_0_3:P c15_1:S q12:V x1_0_2:P x3_0_2:P q10:V x4_0_0:P x6_0_3:P c13_1:S x4_0_1:P x3_0_3:P x4_0_2:P x4_0_3:P q13:V x5_0_0:P o0_0:S x1_0_3:P x2_0_0:P o6_0:V x2_0_1:P x2_0_2:P q15:V o3_0:S x2_0_3:P x5_0_1:P x5_0_2:P x5_0_3:P o4_0:S x7_1_0:P x7_1_1:P x7_0_0:P x7_1_2:P x7_1_3:P o1_0:V x7_0_1:P o2_0:V x7_0_2:P o5_0:V x7_0_3:P o7_1:S o7_0:S"
 
 
 def tile_temporal_log_mel_cepstrum_f4_kernel(
@@ -77,8 +71,9 @@ def tile_temporal_log_mel_cepstrum_f4_kernel(
 
         def load_operand(a):
             if a < 8:
-                g, c = divmod(a, BIN_PASSES)
-                src = power[g * PASS : (g + 1) * PASS, c * PASS : (c + 1) * PASS].rearrange("(m t) k -> m t k", t=PACK)
+                g, h = divmod(a, 2)
+                rows = power[g * PASS : (g + 1) * PASS, :].rearrange("(m t) (c k) -> m t c k", t=PACK, c=BIN_PASSES)
+                src = rows[:, 2 * h : 2 * h + 2].rearrange("m t c k -> m (t c) k")
             else:
                 i = a - 8
                 src = basis[i * P : (i + 1) * P, :].rearrange("q (g k) -> q g k", g=GROUPS)
@@ -106,13 +101,16 @@ def tile_temporal_log_mel_cepstrum_f4_kernel(
         for a in range(4, 16):
             load_operand(a)
 
+        def copier(where):
+            return nc.scalar.copy if where == "S" else nc.vector.tensor_copy
+
         words = {}
         grouped = {}
 
-        def sort_words(a):
+        def sort_words(a, where):
             tile = ring.tile([P, PACK, 2, P], F32, name="sorted", tag="sorted", bufs=4)
             src = raw[a][:].rearrange("p s k -> p (s k)").bitcast(F32)
-            nc.vector.tensor_copy(out=tile[:], in_=src.rearrange("p (s w u) -> p s u w", s=PACK, u=2))
+            copier(where)(out=tile[:], in_=src.rearrange("p (s w u) -> p s u w", s=PACK, u=2))
             words[a] = tile
 
         def turn_operand(a, half):
@@ -120,7 +118,7 @@ def tile_temporal_log_mel_cepstrum_f4_kernel(
             view = bank[:].rearrange("p (s u m) -> p s u m", s=2, u=2)
             src = raw[a][:].rearrange("p s k -> p (s k)").bitcast(F32)
             for s in range(2):
-                slot = 2 * half + s
+                slot = 2 * s + half if a < 8 else 2 * half + s
                 for u in range(2):
                     if a in words:
                         piece = words[a][:, slot, u, :]
@@ -128,11 +126,14 @@ def tile_temporal_log_mel_cepstrum_f4_kernel(
                         piece = src[:, 256 * slot + u : 256 * (slot + 1) : 2]
                     nc.tensor.transpose(view[:, s, u, :], piece, ident[:])
 
-        def gather_operand(a, half):
-            if half == 0:
-                grouped[a] = ring.tile([P, PACK * P * PACK], BF16, name="grouped", tag="grouped", align_bytes=64)
-            dst = grouped[a][:, 1024 * half : 1024 * (half + 1)].bitcast(F32)
-            nc.scalar.copy(
+        def gather_operand(a, half, where):
+            target, part = (a - a % 2 + half, a % 2) if a < 8 else (a, half)
+            if target not in grouped:
+                grouped[target] = ring.tile(
+                    [P, PACK * P * PACK], BF16, name="grouped", tag="grouped", bufs=4, align_bytes=64
+                )
+            dst = grouped[target][:, 1024 * part : 1024 * (part + 1)].bitcast(F32)
+            copier(where)(
                 out=dst.rearrange("p (s m u) -> p s m u", s=2, u=2),
                 in_=last_read(("operand", a, half))[:].rearrange("p (s u m) -> p s m u", s=2, u=2),
             )
@@ -140,9 +141,9 @@ def tile_temporal_log_mel_cepstrum_f4_kernel(
         def quantize_operand(a):
             nc.vector.quantize_mx(out=codes[a][:].bitcast(FP8X4), scales=scales[a][:], in_=grouped[a][:])
 
-        def interleave_filters(c, h):
+        def interleave_filters(c, h, where):
             span = slice(256 * h, 256 * (h + 1))
-            nc.vector.tensor_copy(
+            copier(where)(
                 out=filt_16[c][:, span, :].rearrange("p (n i) j -> p n j i", i=4),
                 in_=filt_raw[c][:, :, span].rearrange("p j (n i) -> p n j i", i=4),
             )
@@ -175,13 +176,12 @@ def tile_temporal_log_mel_cepstrum_f4_kernel(
                 )
 
         def take_log(g, j):
-            logs[g, j] = ring.tile([P, PASS], F32, name="logs", tag="logs")
+            logs[g, j] = ring.tile([P, PASS], F32, name="logs", tag="logs", bufs=4)
             nc.scalar.activation(out=logs[g, j][:], in_=last_read(("energy", g, j))[:], func=ACT.Ln, bias=cols[:, j : j + 1])
 
-        def gain_and_bias(g, j):
+        def gain_and_bias(g, j, where):
             levels[g, j] = ring.tile([P, PASS], F32, name="levels", tag="levels", bufs=6)
-            where = AFFINE_ON[4 * g + j]
-            if where == "s":
+            if where == "S":
                 nc.scalar.activation(
                     out=levels[g, j][:],
                     in_=logs[g, j][:],
@@ -190,7 +190,7 @@ def tile_temporal_log_mel_cepstrum_f4_kernel(
                     bias=cols[:, 8 + j : 9 + j],
                 )
             else:
-                engine = nc.vector if where == "v" else nc.gpsimd
+                engine = nc.vector if where == "V" else nc.gpsimd
                 engine.tensor_scalar(
                     out=levels[g, j][:],
                     in0=logs[g, j][:],
@@ -237,7 +237,7 @@ def tile_temporal_log_mel_cepstrum_f4_kernel(
             width = span.stop - span.start
             bank = last_read(("sums", i, span.start))[:, 0:width]
             result = ring.tile([P, width], F32, name="result", tag="result", bufs=4)
-            if where == "v":
+            if where == "V":
                 nc.vector.tensor_scalar(
                     out=result[:], in0=bank, scalar1=cols[:, 16 + i : 17 + i], scalar2=None, op0=ALU.mult
                 )
@@ -245,77 +245,47 @@ def tile_temporal_log_mel_cepstrum_f4_kernel(
                 nc.scalar.activation(out=result[:], in_=bank, func=ACT.Copy, scale=cols[:, 16 + i : 17 + i])
             nc.sync.dma_start(out=out[i * P : (i + 1) * P, span], in_=result[:])
 
-        def pair(n):
-            g, h = divmod(n, 2)
-            return [(g, 2 * h), (g, 2 * h + 1)] if 0 <= n < 2 * GROUPS else []
+        def piece(i, n):
+            return slice(0, F) if i < QTILES - 1 else slice(256 * n, 256 * (n + 1))
 
-        whole = slice(0, F)
-        every = list(range(GROUPS))
-        second = {
-            10: [(0, whole, [0, 1, 2])],
-            11: [(1, whole, [0, 1, 2])],
-            12: [(2, whole, [0, 1, 2]), (0, whole, [3]), (1, whole, [3]), (2, whole, [3])],
-        }
-        for i in range(3, QTILES - 1):
-            second[10 + i] = [(i, whole, every)]
-        second[17] = [(7, slice(w, w + TAIL), every) for w in range(0, F, TAIL)]
-        finished = []
-
-        for step in range(19):
-            a = step
-            turning = pair(step - LAG_TURN)
-            logging = pair(step - 3)
-            for g, j in logging:
-                take_log(g, j)
-            for g, j in turning:
-                turn_levels(g, j)
-            if step == 1:
-                interleave_filters(0, 0)
-                nc.vector.tensor_copy(out=rows32[:], in_=rows16[:])
-                quantize_filters(0, 0)
-            if a < 16:
-                turn_operand(a, 0)
-                turn_operand(a, 1)
-            if step == 1:
-                bank = take_bank("vectors")
-                nc.tensor.transpose(bank[:, 0:P], rows32[:], ident[:])
-            if 1 <= a <= 16:
-                quantize_operand(a - 1)
-            if step == 1:
-                interleave_filters(0, 1)
-                nc.vector.tensor_copy(out=cols[:], in_=last_read("vectors")[:, 0:32])
-                quantize_filters(0, 1)
-            if step == 2:
-                interleave_filters(1, 0)
-                quantize_filters(1, 0)
-                interleave_filters(1, 1)
-            if step == 3:
-                quantize_filters(1, 1)
-            done_pair = step - LAG_TURN - 1
-            if QH_LATE and done_pair % 2 == 1 and 0 <= done_pair < 2 * GROUPS:
-                quantize_h(done_pair // 2)
-            for n, (i, span) in enumerate(finished):
-                lift_and_store(i, span, LIFT_ON[i] if i < 7 else "sv"[n % 2])
-            finished = []
-            for n in range(2):
-                if turning:
-                    weigh_frames(*turning[n])
-                if logging:
-                    gain_and_bias(*logging[n])
-            if a + SORT_AHEAD in SORTED:
-                sort_words(a + SORT_AHEAD)
-            done_pair = step - LAG_TURN
-            if not QH_LATE and done_pair % 2 == 1 and 0 <= done_pair < 2 * GROUPS:
-                quantize_h(done_pair // 2)
-            if a < 16:
-                gather_operand(a, 0)
-                gather_operand(a, 1)
-            if step in (1, 2):
-                for g, j in pair(step - 1):
-                    mel_matmul(g, j, [0])
-            for g, j in pair(step - 2):
-                mel_matmul(g, j, [1] if step in (2, 3) else [0, 1])
-            for i, span, groups in second.get(step, []):
-                cepstrum_matmul(i, span, groups)
-                if groups[-1] == GROUPS - 1:
-                    finished.append((i, span))
+        for token in ORDER.split():
+            name, where = token.split(":")
+            kind = name[0]
+            if name == "cast":
+                copier(where)(out=rows32[:], in_=rows16[:])
+                continue
+            if name == "tv":
+                nc.tensor.transpose(take_bank("vectors")[:, 0:P], rows32[:], ident[:])
+                continue
+            if name == "cols":
+                copier(where)(out=cols[:], in_=last_read("vectors")[:, 0:32])
+                continue
+            n = list(map(int, name[1:].split("_")))
+            if kind == "s":
+                sort_words(n[0], where)
+            elif kind == "t":
+                turn_operand(n[0], n[1])
+            elif kind == "c":
+                gather_operand(n[0], n[1], where)
+            elif kind == "q":
+                quantize_operand(n[0])
+            elif kind == "i":
+                interleave_filters(n[0], n[1], where)
+            elif kind == "f":
+                quantize_filters(n[0], n[1])
+            elif kind == "m":
+                mel_matmul(n[0], n[1], [n[2]])
+            elif kind == "l":
+                take_log(n[0], n[1])
+            elif kind == "a":
+                gain_and_bias(n[0], n[1], where)
+            elif kind == "u":
+                turn_levels(n[0], n[1])
+            elif kind == "h":
+                weigh_frames(n[0], n[1])
+            elif kind == "H":
+                quantize_h(n[0])
+            elif kind == "x":
+                cepstrum_matmul(n[0], piece(n[0], n[1]), [n[2]])
+            else:
+                lift_and_store(n[0], piece(n[0], n[1]), where)

@@ -23,7 +23,8 @@ BIN_PASSES = K // PASS
 CHUNKS = F // P
 QTILES = Q // P
 BANKS = 8
-ORDER = "t0_1:P c0_1:S i0_1:S cast:V t0_0:P i0_0:V t1_0:P t1_1:P c0_0:V t2_0:P tv:P f0_0:V c1_0:S f0_1:V t2_1:P c1_1:S q0:V i1_0:V c2_0:S q1:V i1_1:S m0_0_0:P f1_0:V m0_2_0:P f1_1:V cols:S t3_1:P t3_0:P m0_1_0:P c2_1:V c3_1:S s4:V c3_0:S m0_2_1:P s5:V l0_2:S m0_0_1:P m0_1_1:P l0_1:S q2:V m0_3_0:P m0_3_1:P t4_0:P t5_1:P a0_2:V t5_0:P l0_3:S t4_1:P c4_0:S c5_0:S s6:V c5_1:S u0_2:P q3:V t6_0:P a0_1:V h0_2:V c4_1:S q4:V a0_3:V s8:V t7_0:P c6_0:S q5:V m1_1_0:P m1_2_0:P m1_3_0:P c7_0:S m1_1_1:P m1_0_0:P m1_3_1:P m1_0_1:P l1_1:S m1_2_1:P l1_3:S t6_1:P t7_1:P l1_0:S c7_1:S t9_0:P u0_1:P l1_2:S a1_1:V c6_1:V a1_3:V t8_0:P t9_1:P u0_3:P c9_0:S a1_0:V u1_3:P h0_1:V u1_0:P q7:V l0_0:S a1_2:V c9_1:S t8_1:P q6:V m2_0_0:P h1_3:V c8_0:S m2_1_0:P m2_1_1:P c8_1:S m3_0_0:P l2_1:S m3_2_0:P m2_2_0:P m2_0_1:P m3_2_1:P a0_0:S m3_0_1:P s11:V h1_0:V l2_0:S m2_2_1:P q9:V m2_3_0:P m3_3_0:P m3_1_0:P a2_1:V m3_1_1:P m3_3_1:P l3_0:S u1_1:P u1_2:P l2_2:S l3_2:S h0_3:V m2_3_1:P s15:V t11_0:P q8:V a2_2:V a2_0:V a3_0:S h1_1:V u0_0:P l2_3:S h1_2:V u2_0:P l3_3:S t12_1:P c11_0:S a3_2:V t11_1:P h2_0:V h0_0:V c11_1:S l3_1:S u3_0:P a2_3:S u3_2:P h3_0:V h3_2:V u2_1:P q11:V t14_1:P t12_0:P t14_0:P u2_2:P c14_1:S c12_0:S t15_0:P t10_0:P a3_3:S t10_1:P h2_1:V h2_2:V H0:V c15_0:S u2_3:P u3_3:P h2_3:V a3_1:S t15_1:P t13_1:P c14_0:S h3_3:V c12_1:S H1:V u3_1:P c10_0:S q14:V h3_1:V t13_0:P x3_0_0:P x3_0_1:P x1_0_0:P H2:V x6_0_0:P x6_0_1:P x1_0_1:P c10_1:S x0_0_0:P H3:V x0_0_1:P x0_0_2:P c13_0:S x6_0_2:P x0_0_3:P c15_1:S q12:V x1_0_2:P x3_0_2:P q10:V x4_0_0:P x6_0_3:P c13_1:S x4_0_1:P x3_0_3:P x4_0_2:P x4_0_3:P q13:V x5_0_0:P o0_0:S x1_0_3:P x2_0_0:P o6_0:V x2_0_1:P x2_0_2:P q15:V o3_0:S x2_0_3:P x5_0_1:P x5_0_2:P x5_0_3:P o4_0:S x7_1_0:P x7_1_1:P x7_0_0:P x7_1_2:P x7_1_3:P o1_0:V x7_0_1:P o2_0:V x7_0_2:P o5_0:V x7_0_3:P o7_1:S o7_0:S"
+ORDER = "t0_0:P i0_0:V t0_1:P i0_1:S f0_0:V c0_0:S c0_1:S t1_0:P f0_1:V c1_0:V cast:V q0:V t1_1:P c1_1:S t2_0:P c2_0:S q1:V t2_1:P i1_0:S tv:P m0_0_0:P c2_1:S cols:V m0_1_0:P i1_1:V t3_0:P t3_1:P c3_0:S f1_0:V c3_1:S f1_1:V m0_0_1:P m0_2_0:P s4:V l0_0:S q2:V m0_1_1:P m0_2_1:P q3:V m0_3_0:P m0_3_1:P m1_0_0:P m1_1_0:P m1_0_1:P m1_1_1:P a0_0:V l0_1:S l0_2:S s5:V a0_1:V a0_2:V s6:V l0_3:S m1_2_0:P l1_0:S m1_2_1:P a0_3:V u0_0:P l1_1:S l1_2:S s7:V t4_0:P h0_0:V t4_1:P t5_0:P u0_1:P a1_0:V c4_0:S u0_2:P c4_1:S t5_1:P t6_0:P h0_1:V c5_0:S t6_1:P u0_3:P t7_0:P t7_1:P h0_2:V u1_0:P c5_1:S t8_0:P c6_0:S c6_1:S a1_1:V c7_0:S t8_1:P a1_2:V u1_1:P q4:V m1_3_0:P m1_3_1:P h0_3:V c7_1:S q5:V m2_0_0:P m2_1_0:P h1_0:V c8_0:S m2_0_1:P m2_2_0:P H0:V m2_1_1:P l1_3:S m2_3_0:P m2_2_1:P q6:V l2_0:S m2_3_1:P m3_0_0:P u1_2:P l2_1:S t9_0:P a1_3:V q7:V c8_1:S l2_2:S a2_0:V a2_1:V h1_1:V h1_2:V u1_3:P t9_1:P u2_0:P l2_3:S c9_0:S h1_3:V a2_2:S u2_1:P q8:V t10_0:P c9_1:S m3_0_1:P m3_1_0:P l3_0:S H1:V m3_1_1:P s11:V x0_0_0:P m3_2_0:P m3_2_1:P c10_0:S h2_0:V a2_3:V x0_0_1:P t10_1:P l3_1:S a3_0:S t11_0:P h2_1:V u2_2:P l3_2:S u2_3:P q9:V s12:V h2_2:V u3_0:P m3_3_0:P x1_0_0:P m3_3_1:P x1_0_1:P t11_1:P c10_1:S a3_1:S h2_3:V l3_3:S h3_0:V u3_1:P t12_0:P t12_1:P t13_0:P a3_2:V c11_0:S h3_1:V u3_2:P c11_1:S a3_3:S t13_1:P H2:V u3_3:P q10:V c12_0:S x0_0_2:P x2_0_0:P x2_0_1:P c12_1:S x1_0_2:P x2_0_2:P h3_2:V s14:V h3_3:V s15:S H3:V t14_0:P t14_1:P c13_0:S c13_1:S t15_0:P q11:V c14_0:S t15_1:P x0_0_3:P q12:V x1_0_3:P q13:V x2_0_3:P o0_0:S o1_0:S x3_0_0:P x3_0_1:P x3_0_2:P c14_1:S x3_0_3:P c15_0:V x4_0_0:P x4_0_1:P x5_0_0:P o2_0:V x4_0_2:P q14:V o3_0:S c15_1:S x4_0_3:P x5_0_1:P x5_0_2:P x5_0_3:P o4_0:V x6_0_0:P o5_0:S q15:V x6_0_1:P x6_0_2:P x6_0_3:P x7_0_0:P x7_0_1:P x7_1_0:P x7_0_2:P x7_0_3:P o6_0:V x7_1_1:P x7_1_2:P x7_1_3:P o7_0:S o7_1:V"
+LOADS = "f0 r0 r1 r2 vec f1 r3 r4 w r5 r6 r7 r8 r9 r10 r11 r12 r13 r14 r15"
 
 
 def tile_temporal_log_mel_cepstrum_f4_kernel(
@@ -84,22 +85,21 @@ def tile_temporal_log_mel_cepstrum_f4_kernel(
             nc.sync.dma_start(out=filt_raw[c][:], in_=src.rearrange("(p j) f -> p j f", j=PACK))
 
         make_identity(nc, ident[:])
-        nc.vector.memset(rows16[:], 0.0)
         nc.vector.memset(one[:], 1.0)
-        load_operand(0)
-        load_filters(0)
-        nc.scalar.dma_start(out=rows16[0:4, :], in_=offset.rearrange("(j p) -> j p", p=P))
-        nc.scalar.dma_start(out=rows16[4:8, :], in_=gain.rearrange("(j p) -> j p", p=P))
-        nc.scalar.dma_start(out=rows16[8:12, :], in_=bias.rearrange("(j p) -> j p", p=P))
-        nc.scalar.dma_start(out=rows16[16:24, :], in_=lifter.rearrange("(i p) -> i p", p=P))
+        nc.vector.memset(rows16[:], 0.0)
         nc.scalar.activation(out=warm[:], in_=one[:], func=ACT.Ln)
-        load_operand(1)
-        load_operand(2)
-        load_filters(1)
-        load_operand(3)
-        nc.sync.dma_start(out=weight[:], in_=frame_weight.rearrange("(g m t) -> m g t", m=P, t=PACK))
-        for a in range(4, 16):
-            load_operand(a)
+        for name in LOADS.split():
+            if name == "w":
+                nc.sync.dma_start(out=weight[:], in_=frame_weight.rearrange("(g m t) -> m g t", m=P, t=PACK))
+            elif name == "vec":
+                nc.scalar.dma_start(out=rows16[0:4, :], in_=offset.rearrange("(j p) -> j p", p=P))
+                nc.scalar.dma_start(out=rows16[4:8, :], in_=gain.rearrange("(j p) -> j p", p=P))
+                nc.scalar.dma_start(out=rows16[8:12, :], in_=bias.rearrange("(j p) -> j p", p=P))
+                nc.scalar.dma_start(out=rows16[16:24, :], in_=lifter.rearrange("(i p) -> i p", p=P))
+            elif name[0] == "f":
+                load_filters(int(name[1:]))
+            else:
+                load_operand(int(name[1:]))
 
         def copier(where):
             return nc.scalar.copy if where == "S" else nc.vector.tensor_copy

@@ -17,23 +17,76 @@ ALU = mybir.AluOpType
 P = 128
 PACK = 4
 PASS = P * PACK
+PASS_WORDS = PASS // 2
 BANK = 512
+BANKS = 8
 GROUPS = T // PASS
 BIN_PASSES = K // PASS
-CHUNKS = F // P
-QTILES = Q // P
-BANKS = 8
-ORDER = "t0_0:P i0_0:V t0_1:P i0_1:S f0_0:V c0_0:S c0_1:S t1_0:P f0_1:V c1_0:V cast:V q0:V t1_1:P c1_1:S t2_0:P c2_0:S q1:V t2_1:P i1_0:S tv:P m0_0_0:P c2_1:S cols:V m0_1_0:P i1_1:V t3_0:P t3_1:P c3_0:S f1_0:V c3_1:S f1_1:V m0_0_1:P m0_2_0:P s4:V l0_0:S q2:V m0_1_1:P m0_2_1:P q3:V m0_3_0:P m0_3_1:P m1_0_0:P m1_1_0:P m1_0_1:P m1_1_1:P a0_0:V l0_1:S l0_2:S s5:V a0_1:V a0_2:V s6:V l0_3:S m1_2_0:P l1_0:S m1_2_1:P a0_3:V u0_0:P l1_1:S l1_2:S s7:V t4_0:P h0_0:V t4_1:P t5_0:P u0_1:P a1_0:V c4_0:S u0_2:P c4_1:S t5_1:P t6_0:P h0_1:V c5_0:S t6_1:P u0_3:P t7_0:P t7_1:P h0_2:V u1_0:P c5_1:S t8_0:P c6_0:S c6_1:S a1_1:V c7_0:S t8_1:P a1_2:V u1_1:P q4:V m1_3_0:P m1_3_1:P h0_3:V c7_1:S q5:V m2_0_0:P m2_1_0:P h1_0:V c8_0:S m2_0_1:P m2_2_0:P H0:V m2_1_1:P l1_3:S m2_3_0:P m2_2_1:P q6:V l2_0:S m2_3_1:P m3_0_0:P u1_2:P l2_1:S t9_0:P a1_3:V q7:V c8_1:S l2_2:S a2_0:V a2_1:V h1_1:V h1_2:V u1_3:P t9_1:P u2_0:P l2_3:S c9_0:S h1_3:V a2_2:S u2_1:P q8:V t10_0:P c9_1:S m3_0_1:P m3_1_0:P l3_0:S H1:V m3_1_1:P s11:V x0_0_0:P m3_2_0:P m3_2_1:P c10_0:S h2_0:V a2_3:V x0_0_1:P t10_1:P l3_1:S a3_0:S t11_0:P h2_1:V u2_2:P l3_2:S u2_3:P q9:V s12:V h2_2:V u3_0:P m3_3_0:P x1_0_0:P m3_3_1:P x1_0_1:P t11_1:P c10_1:S a3_1:S h2_3:V l3_3:S h3_0:V u3_1:P t12_0:P t12_1:P t13_0:P a3_2:V c11_0:S h3_1:V u3_2:P c11_1:S a3_3:S t13_1:P H2:V u3_3:P q10:V c12_0:S x0_0_2:P x2_0_0:P x2_0_1:P c12_1:S x1_0_2:P x2_0_2:P h3_2:V s14:V h3_3:V s15:S H3:V t14_0:P t14_1:P c13_0:S c13_1:S t15_0:P q11:V c14_0:S t15_1:P x0_0_3:P q12:V x1_0_3:P q13:V x2_0_3:P o0_0:S o1_0:S x3_0_0:P x3_0_1:P x3_0_2:P c14_1:S x3_0_3:P c15_0:V x4_0_0:P x4_0_1:P x5_0_0:P o2_0:V x4_0_2:P q14:V o3_0:S c15_1:S x4_0_3:P x5_0_1:P x5_0_2:P x5_0_3:P o4_0:V x6_0_0:P o5_0:S q15:V x6_0_1:P x6_0_2:P x6_0_3:P x7_0_0:P x7_0_1:P x7_1_0:P x7_0_2:P x7_0_3:P o6_0:V x7_1_1:P x7_1_2:P x7_1_3:P o7_0:S o7_1:V"
-LOADS = "f0 r0 r1 r2 vec f1 r3 r4 w r5 r6 r7 r8 r9 r10 r11 r12 r13 r14 r15"
+ROW_TILES = Q // P
+HALF = F // 2
+
+POWER_SOURCES = 2 * GROUPS
+SOURCES = POWER_SOURCES + ROW_TILES
+
+OFFSET_AT, GAIN_AT, BIAS_AT, LIFTER_AT, VECTOR_COLUMNS = 0, 4, 8, 16, 32
+
+SORTED_BUFS, PACKED_BUFS, LOG_BUFS, LEVEL_BUFS, RESULT_BUFS = 4, 4, 4, 6, 4
+
+LOADS = """
+load_filters:0 load_source:0 load_vectors load_source:1 load_source:2 load_source:3 load_filters:1 load_weight
+load_source:4 load_source:5 load_source:6 load_source:7 load_source:8 load_source:9 load_source:10
+load_source:11 load_source:12 load_source:13 load_source:14 load_source:15
+"""
+
+SCHEDULE = """
+pack_filters:0:0:V quantize_filters:0:0 pack_filters:0:1:V turn_source:0:0 turn_source:0:1 turn_source:1:0
+    pack:0:0:S pack:0:1:V quantize_filters:0:1 pack:1:0:S turn_source:1:1 pack:1:1:S turn_source:2:0
+    turn_source:2:1 widen_vectors quantize:0 turn_vectors turn_source:3:0 quantize:1 pack_filters:1:0:V
+    pack:2:0:S pack:2:1:S pack:3:0:S pack_filters:1:1:S
+mel:0:0:0 quantize_filters:1:0
+turn_source:3:1 keep_vectors:S quantize:2
+mel:0:1:0 mel:0:2:0 mel:0:0:1 quantize_filters:1:1 mel:0:3:0 pack:3:1:S log:0:0 sort_words:4:V mel:0:1:1
+    mel:1:0:0 mel:0:2:1 sort_words:5:V mel:0:3:1
+turn_source:4:0 log:0:1 level:0:0:S quantize:3 sort_words:6:V turn_source:4:1 turn_source:5:0 level:0:1:G
+    turn_source:5:1 log:0:2 turn_levels:0:0 turn_source:6:0 log:0:3 pack:4:0:S pack:4:1:V pack:5:0:V
+    sort_words:7:S pack:5:1:V pack:6:0:V
+mel:1:0:1 mel:1:1:0 mel:1:1:1 log:1:0 log:1:1 mel:1:2:0 quantize:4 mel:1:2:1 mel:1:3:0 level:0:2:G mel:1:3:1
+turn_levels:0:1 log:1:2 turn_source:6:1 level:0:3:G quantize:5 turn_source:7:0 log:1:3 sort_words:9:V
+    turn_levels:0:2 weigh:0:0 pack:6:1:V turn_source:7:1 weigh:0:1 pack:7:0:S level:1:0:G turn_source:8:0
+    level:1:1:S turn_source:8:1 pack:7:1:S
+mel:2:0:0 mel:2:0:1 pack:8:0:S mel:2:1:0 mel:2:2:0 weigh:0:2 level:1:2:G quantize:6 mel:2:3:0 mel:2:1:1 log:2:0
+    sort_words:10:V mel:2:2:1 quantize:7 mel:2:3:1 mel:3:0:0 mel:3:0:1 sort_words:11:V
+turn_levels:0:3 pack:8:1:S turn_source:9:0 log:2:1 sort_words:12:V quantize:8 turn_levels:1:0 log:2:2
+    level:1:3:G turn_levels:1:1 weigh:0:3 turn_source:9:1 turn_levels:1:2 log:2:3 level:2:0:G weigh:1:0
+    turn_source:10:0 turn_source:10:1 weigh:1:1 turn_levels:1:3 level:2:1:G pack:9:0:S pack:9:1:S
+mel:3:1:0 sort_words:13:S weigh:1:2 weigh:1:3 pack:10:0:S sort_words:14:V quantize_h:0 mel:3:2:0 mel:3:1:1
+    pack:10:1:S mel:3:3:0 level:2:2:G mel:3:2:1 mel:3:3:1
+turn_levels:2:0 log:3:0 turn_levels:2:1 level:2:3:G log:3:1 turn_levels:2:2 turn_source:11:0 quantize:9
+    weigh:2:0 turn_levels:2:3 weigh:2:1 turn_source:11:1 level:3:0:G turn_levels:3:0 level:3:1:G
+    turn_source:12:0 log:3:2 turn_source:12:1 weigh:2:2 turn_levels:3:1 log:3:3 pack:11:0:S level:3:2:G
+    turn_levels:3:2 weigh:2:3 pack:11:1:S weigh:3:0 sort_words:15:S weigh:3:1 weigh:3:2 turn_source:13:0
+    turn_source:13:1 turn_source:14:0 level:3:3:G pack:12:0:S quantize_h:1 turn_source:14:1 turn_source:15:0
+    turn_source:15:1 quantize_h:2 turn_levels:3:3 pack:12:1:S
+cepstrum:0:0:0 quantize:10 cepstrum:0:0:1 pack:13:0:S weigh:3:3 quantize:11 cepstrum:1:0:0 cepstrum:0:0:2
+    cepstrum:1:0:1 pack:13:1:S cepstrum:1:0:2 cepstrum:2:0:0 cepstrum:2:0:1 quantize_h:3 cepstrum:3:0:0
+    cepstrum:3:0:1 cepstrum:0:0:3 pack:14:0:S cepstrum:1:0:3 quantize:12 cepstrum:2:0:2 store:0:0:S quantize:13
+    pack:14:1:S cepstrum:2:0:3 cepstrum:3:0:2 cepstrum:4:0:0 cepstrum:5:0:0 cepstrum:4:0:1 store:1:0:V
+    cepstrum:3:0:3 store:2:0:V quantize:14 cepstrum:4:0:2 cepstrum:4:0:3 pack:15:0:S pack:15:1:V cepstrum:5:0:1
+    cepstrum:6:0:0 store:3:0:S cepstrum:5:0:2 store:4:0:V quantize:15 cepstrum:5:0:3 cepstrum:6:0:1 store:5:0:S
+    cepstrum:6:0:2 cepstrum:6:0:3 cepstrum:7:0:0 cepstrum:7:1:0 cepstrum:7:0:1 cepstrum:7:0:2 cepstrum:7:0:3
+    store:6:0:V cepstrum:7:1:1 store:7:0:V cepstrum:7:1:2 cepstrum:7:1:3 store:7:1:V
+"""
 
 
 def tile_temporal_log_mel_cepstrum_f4_kernel(
     tc, power, filters, offset, gain, bias, frame_weight, basis, lifter, out
 ):
     nc = tc.nc
+    copy_on = {"V": nc.vector.tensor_copy, "S": nc.scalar.copy}
+
     with ExitStack() as ctx:
         keep = ctx.enter_context(tc.tile_pool(name="keep", bufs=1))
-        ring = ctx.enter_context(tc.tile_pool(name="ring", bufs=3))
+        ring = ctx.enter_context(tc.tile_pool(name="ring", bufs=1))
         psum = ctx.enter_context(tc.psum_pool(name="psum", bufs=1))
         ctx.enter_context(tc.manual_schedule())
 
@@ -44,248 +97,256 @@ def tile_temporal_log_mel_cepstrum_f4_kernel(
             tag = idle_banks[0]
             idle_banks.remove(tag)
             held[use] = (tag, psum.tile([P, BANK], F32, name=tag, tag=tag))
+
+        def bank_of(use):
             return held[use][1]
 
-        def last_read(use):
-            tag, bank = held[use]
-            idle_banks.append(tag)
-            return bank
+        def give_back(use):
+            idle_banks.append(held[use][0])
 
         ident = keep.tile([P, P], F32, name="ident")
-        rows16 = keep.tile([P, P], BF16, name="rows16")
-        rows32 = keep.tile([P, P], F32, name="rows32")
-        cols = keep.tile([P, 32], F32, name="cols")
-        one = keep.tile([P, 1], F32, name="one")
-        warm = keep.tile([P, 1], F32, name="warm")
+        vector_rows16 = keep.tile([P, P], BF16, name="vector_rows16")
+        vector_rows32 = keep.tile([P, P], F32, name="vector_rows32")
+        vectors = keep.tile([P, VECTOR_COLUMNS], F32, name="vectors")
         weight = keep.tile([P, GROUPS, PACK], BF16, name="weight")
 
-        raw = [keep.tile([P, PACK, PASS], BF16, name="raw%d" % a) for a in range(16)]
-        codes = [keep.tile([P, PASS], U32, name="codes%d" % a, align_bytes=64) for a in range(16)]
-        scales = [keep.tile([P, PASS], U8, name="scales%d" % a, align_bytes=64) for a in range(16)]
-        filt_raw = [keep.tile([P, PACK, F], BF16, name="filt_raw%d" % c) for c in range(BIN_PASSES)]
-        filt_16 = [keep.tile([P, F, PACK], BF16, name="filt_16_%d" % c, align_bytes=64) for c in range(BIN_PASSES)]
-        filt_codes = [keep.tile([P, F], U32, name="filt_codes%d" % c, align_bytes=64) for c in range(BIN_PASSES)]
-        filt_scales = [keep.tile([P, F], U8, name="filt_scales%d" % c, align_bytes=64) for c in range(BIN_PASSES)]
-        h16 = [keep.tile([P, F, PACK], BF16, name="h16_%d" % g, align_bytes=64) for g in range(GROUPS)]
-        h_codes = [keep.tile([P, F], U32, name="h_codes%d" % g, align_bytes=64) for g in range(GROUPS)]
-        h_scales = [keep.tile([P, F], U8, name="h_scales%d" % g, align_bytes=64) for g in range(GROUPS)]
+        def mx_tiles(name, count, width):
+            code_tiles = [keep.tile([P, width], U32, name="%s_codes%d" % (name, n), align_bytes=64) for n in range(count)]
+            scale_tiles = [keep.tile([P, width], U8, name="%s_scales%d" % (name, n), align_bytes=64) for n in range(count)]
+            return code_tiles, scale_tiles
 
-        def load_operand(a):
-            if a < 8:
-                g, h = divmod(a, 2)
+        source = [keep.tile([P, PACK, PASS], BF16, name="source%d" % a) for a in range(SOURCES)]
+        codes, scales = mx_tiles("operand", SOURCES, PASS)
+        filter_rows = [keep.tile([P, PACK, F], BF16, name="filter_rows%d" % c) for c in range(BIN_PASSES)]
+        filter_16 = [keep.tile([P, F, PACK], BF16, name="filter_16_%d" % c, align_bytes=64) for c in range(BIN_PASSES)]
+        filter_codes, filter_scales = mx_tiles("filter", BIN_PASSES, F)
+        h_16 = [keep.tile([P, F, PACK], BF16, name="h_16_%d" % g, align_bytes=64) for g in range(GROUPS)]
+        h_codes, h_scales = mx_tiles("h", GROUPS, F)
+
+        def vector_column(first, n):
+            return vectors[:, first + n : first + n + 1]
+
+        def chunk(j):
+            return slice(j * P, (j + 1) * P)
+
+        def half(n):
+            return slice(n * HALF, (n + 1) * HALF)
+
+
+        def load_source(a):
+            if a < POWER_SOURCES:
+                g, r = divmod(a, 2)
                 rows = power[g * PASS : (g + 1) * PASS, :].rearrange("(m t) (c k) -> m t c k", t=PACK, c=BIN_PASSES)
-                src = rows[:, 2 * h : 2 * h + 2].rearrange("m t c k -> m (t c) k")
+                src = rows[:, 2 * r : 2 * r + 2].rearrange("m t c k -> m (t c) k")
             else:
-                i = a - 8
-                src = basis[i * P : (i + 1) * P, :].rearrange("q (g k) -> q g k", g=GROUPS)
-            nc.sync.dma_start(out=raw[a][:], in_=src)
+                src = basis[chunk(a - POWER_SOURCES), :].rearrange("q (g k) -> q g k", g=GROUPS)
+            nc.sync.dma_start(out=source[a][:], in_=src)
 
         def load_filters(c):
-            src = filters[c * PASS : (c + 1) * PASS, :]
-            nc.sync.dma_start(out=filt_raw[c][:], in_=src.rearrange("(p j) f -> p j f", j=PACK))
+            src = filters[c * PASS : (c + 1) * PASS, :].rearrange("(p t) f -> p t f", t=PACK)
+            nc.sync.dma_start(out=filter_rows[c][:], in_=src)
 
-        make_identity(nc, ident[:])
-        nc.vector.memset(one[:], 1.0)
-        nc.vector.memset(rows16[:], 0.0)
-        nc.scalar.activation(out=warm[:], in_=one[:], func=ACT.Ln)
-        for name in LOADS.split():
-            if name == "w":
-                nc.sync.dma_start(out=weight[:], in_=frame_weight.rearrange("(g m t) -> m g t", m=P, t=PACK))
-            elif name == "vec":
-                nc.scalar.dma_start(out=rows16[0:4, :], in_=offset.rearrange("(j p) -> j p", p=P))
-                nc.scalar.dma_start(out=rows16[4:8, :], in_=gain.rearrange("(j p) -> j p", p=P))
-                nc.scalar.dma_start(out=rows16[8:12, :], in_=bias.rearrange("(j p) -> j p", p=P))
-                nc.scalar.dma_start(out=rows16[16:24, :], in_=lifter.rearrange("(i p) -> i p", p=P))
-            elif name[0] == "f":
-                load_filters(int(name[1:]))
-            else:
-                load_operand(int(name[1:]))
+        def load_weight():
+            nc.sync.dma_start(out=weight[:], in_=frame_weight.rearrange("(g p t) -> p g t", p=P, t=PACK))
 
-        def copier(where):
-            return nc.scalar.copy if where == "S" else nc.vector.tensor_copy
+        def load_vectors():
+            for vector, first in ((offset, OFFSET_AT), (gain, GAIN_AT), (bias, BIAS_AT), (lifter, LIFTER_AT)):
+                rows = vector.rearrange("(j p) -> j p", p=P)
+                nc.scalar.dma_start(out=vector_rows16[first : first + rows.shape[0], :], in_=rows)
 
-        words = {}
-        grouped = {}
 
-        def sort_words(a, where):
-            tile = ring.tile([P, PACK, 2, P], F32, name="sorted", tag="sorted", bufs=4)
-            src = raw[a][:].rearrange("p s k -> p (s k)").bitcast(F32)
-            copier(where)(out=tile[:], in_=src.rearrange("p (s w u) -> p s u w", s=PACK, u=2))
-            words[a] = tile
+        def widen_vectors():
+            nc.vector.tensor_copy(out=vector_rows32[:], in_=vector_rows16[:])
 
-        def turn_operand(a, half):
-            bank = take_bank(("operand", a, half))
-            view = bank[:].rearrange("p (s u m) -> p s u m", s=2, u=2)
-            src = raw[a][:].rearrange("p s k -> p (s k)").bitcast(F32)
-            for s in range(2):
-                slot = 2 * s + half if a < 8 else 2 * half + s
+        def turn_vectors():
+            take_bank("vectors")
+            nc.tensor.transpose(bank_of("vectors")[:, 0:P], vector_rows32[:], ident[:])
+
+        def keep_vectors(engine):
+            copy_on[engine](out=vectors[:], in_=bank_of("vectors")[:, 0:VECTOR_COLUMNS])
+            give_back("vectors")
+
+
+        sorted_words = {}
+        packed = {}
+
+        def words_of(a):
+            return source[a][:].rearrange("p s k -> p (s k)").bitcast(F32)
+
+        def sort_words(a, engine):
+            sorted_words[a] = ring.tile([P, PACK, 2, P], F32, name="sorted", tag="sorted", bufs=SORTED_BUFS)
+            copy_on[engine](out=sorted_words[a][:], in_=words_of(a).rearrange("p (s w u) -> p s u w", s=PACK, u=2))
+
+        def turn_source(a, b):
+            take_bank(("source", a, b))
+            view = bank_of(("source", a, b))[:].rearrange("p (n u m) -> p n u m", n=2, u=2)
+            for n in range(2):
+                s = 2 * n + b if a < POWER_SOURCES else 2 * b + n
                 for u in range(2):
-                    if a in words:
-                        piece = words[a][:, slot, u, :]
+                    if a in sorted_words:
+                        piece = sorted_words[a][:, s, u, :]
                     else:
-                        piece = src[:, 256 * slot + u : 256 * (slot + 1) : 2]
-                    nc.tensor.transpose(view[:, s, u, :], piece, ident[:])
+                        piece = words_of(a)[:, PASS_WORDS * s + u : PASS_WORDS * (s + 1) : 2]
+                    nc.tensor.transpose(view[:, n, u, :], piece, ident[:])
 
-        def gather_operand(a, half, where):
-            target, part = (a - a % 2 + half, a % 2) if a < 8 else (a, half)
-            if target not in grouped:
-                grouped[target] = ring.tile(
-                    [P, PACK * P * PACK], BF16, name="grouped", tag="grouped", bufs=4, align_bytes=64
+        def pack(a, b, engine):
+            if a < POWER_SOURCES:
+                g, part = divmod(a, 2)
+                operand = BIN_PASSES * g + b
+            else:
+                operand, part = a, b
+            if operand not in packed:
+                packed[operand] = ring.tile(
+                    [P, PASS * PACK], BF16, name="packed", tag="packed", bufs=PACKED_BUFS, align_bytes=64
                 )
-            dst = grouped[target][:, 1024 * part : 1024 * (part + 1)].bitcast(F32)
-            copier(where)(
-                out=dst.rearrange("p (s m u) -> p s m u", s=2, u=2),
-                in_=last_read(("operand", a, half))[:].rearrange("p (s u m) -> p s m u", s=2, u=2),
+            dst = packed[operand][:].bitcast(F32)[:, BANK * part : BANK * (part + 1)]
+            copy_on[engine](
+                out=dst.rearrange("p (n m u) -> p n m u", n=2, u=2),
+                in_=bank_of(("source", a, b))[:].rearrange("p (n u m) -> p n m u", n=2, u=2),
+            )
+            give_back(("source", a, b))
+
+        def quantize(operand):
+            nc.vector.quantize_mx(out=codes[operand][:].bitcast(FP8X4), scales=scales[operand][:], in_=packed[operand][:])
+
+
+        def pack_filters(c, n, engine):
+            copy_on[engine](
+                out=filter_16[c][:, half(n), :].rearrange("p (f i) t -> p f t i", i=PACK),
+                in_=filter_rows[c][:, :, half(n)].rearrange("p t (f i) -> p f t i", i=PACK),
             )
 
-        def quantize_operand(a):
-            nc.vector.quantize_mx(out=codes[a][:].bitcast(FP8X4), scales=scales[a][:], in_=grouped[a][:])
-
-        def interleave_filters(c, h, where):
-            span = slice(256 * h, 256 * (h + 1))
-            copier(where)(
-                out=filt_16[c][:, span, :].rearrange("p (n i) j -> p n j i", i=4),
-                in_=filt_raw[c][:, :, span].rearrange("p j (n i) -> p n j i", i=4),
-            )
-
-        def quantize_filters(c, h):
-            span = slice(256 * h, 256 * (h + 1))
+        def quantize_filters(c, n):
             nc.vector.quantize_mx(
-                out=filt_codes[c][:, span].bitcast(FP8X4),
-                scales=filt_scales[c][:, span],
-                in_=filt_16[c][:, span, :].rearrange("p f j -> p (f j)"),
+                out=filter_codes[c][:, half(n)].bitcast(FP8X4),
+                scales=filter_scales[c][:, half(n)],
+                in_=filter_16[c][:, half(n), :].rearrange("p f t -> p (f t)"),
             )
+
 
         logs = {}
         levels = {}
 
-        def mel_matmul(g, j, passes):
-            if passes[0] == 0:
+        def mel(g, j, c):
+            if c == 0:
                 take_bank(("energy", g, j))
-            bank = held["energy", g, j][1]
-            for c in passes:
-                a = BIN_PASSES * g + c
-                nc.tensor.matmul_mx(
-                    out=bank[:],
-                    lhsT=filt_codes[c][:, j * P : (j + 1) * P].bitcast(FP8X4),
-                    lhsT_scale=filt_scales[c][:, j * P : (j + 1) * P],
-                    rhs=codes[a][:].bitcast(FP8X4),
-                    rhs_scale=scales[a][:],
-                    start=(c == 0),
-                    stop=(c == BIN_PASSES - 1),
-                )
+            operand = BIN_PASSES * g + c
+            nc.tensor.matmul_mx(
+                out=bank_of(("energy", g, j))[:],
+                lhsT=filter_codes[c][:, chunk(j)].bitcast(FP8X4),
+                lhsT_scale=filter_scales[c][:, chunk(j)],
+                rhs=codes[operand][:].bitcast(FP8X4),
+                rhs_scale=scales[operand][:],
+                start=(c == 0),
+                stop=(c == BIN_PASSES - 1),
+            )
 
-        def take_log(g, j):
-            logs[g, j] = ring.tile([P, PASS], F32, name="logs", tag="logs", bufs=4)
-            nc.scalar.activation(out=logs[g, j][:], in_=last_read(("energy", g, j))[:], func=ACT.Ln, bias=cols[:, j : j + 1])
+        def log(g, j):
+            logs[g, j] = ring.tile([P, PASS], F32, name="logs", tag="logs", bufs=LOG_BUFS)
+            nc.scalar.activation(
+                out=logs[g, j][:], in_=bank_of(("energy", g, j))[:], func=ACT.Ln, bias=vector_column(OFFSET_AT, j)
+            )
+            give_back(("energy", g, j))
 
-        def gain_and_bias(g, j, where):
-            levels[g, j] = ring.tile([P, PASS], F32, name="levels", tag="levels", bufs=6)
-            if where == "S":
+        def level(g, j, engine):
+            levels[g, j] = ring.tile([P, PASS], F32, name="levels", tag="levels", bufs=LEVEL_BUFS)
+            if engine == "S":
                 nc.scalar.activation(
                     out=levels[g, j][:],
                     in_=logs[g, j][:],
                     func=ACT.Identity,
-                    scale=cols[:, 4 + j : 5 + j],
-                    bias=cols[:, 8 + j : 9 + j],
+                    scale=vector_column(GAIN_AT, j),
+                    bias=vector_column(BIAS_AT, j),
                 )
             else:
-                engine = nc.vector if where == "V" else nc.gpsimd
-                engine.tensor_scalar(
+                nc.gpsimd.tensor_scalar(
                     out=levels[g, j][:],
                     in0=logs[g, j][:],
-                    scalar1=cols[:, 4 + j : 5 + j],
-                    scalar2=cols[:, 8 + j : 9 + j],
+                    scalar1=vector_column(GAIN_AT, j),
+                    scalar2=vector_column(BIAS_AT, j),
                     op0=ALU.mult,
                     op1=ALU.add,
                 )
 
         def turn_levels(g, j):
-            bank = take_bank(("levels", g, j))
+            take_bank(("levels", g, j))
             for t in range(PACK):
-                nc.tensor.transpose(bank[:, t * P : (t + 1) * P], levels[g, j][:, t * P : (t + 1) * P], ident[:])
+                nc.tensor.transpose(bank_of(("levels", g, j))[:, chunk(t)], levels[g, j][:, chunk(t)], ident[:])
 
-        def weigh_frames(g, j):
+        def weigh(g, j):
             nc.vector.tensor_tensor(
-                out=h16[g][:, j * P : (j + 1) * P, :],
-                in0=last_read(("levels", g, j))[:].rearrange("p (t f) -> p f t", t=PACK),
+                out=h_16[g][:, chunk(j), :],
+                in0=bank_of(("levels", g, j))[:].rearrange("p (t f) -> p f t", t=PACK),
                 in1=weight[:, g, :].unsqueeze(1).broadcast_to([P, P, PACK]),
                 op=ALU.mult,
             )
+            give_back(("levels", g, j))
 
         def quantize_h(g):
             nc.vector.quantize_mx(
-                out=h_codes[g][:].bitcast(FP8X4), scales=h_scales[g][:], in_=h16[g][:].rearrange("p f t -> p (f t)")
+                out=h_codes[g][:].bitcast(FP8X4), scales=h_scales[g][:], in_=h_16[g][:].rearrange("p f t -> p (f t)")
             )
 
-        def cepstrum_matmul(i, span, groups):
-            if groups[0] == 0:
-                take_bank(("sums", i, span.start))
-            bank = held["sums", i, span.start][1]
-            for g in groups:
-                nc.tensor.matmul_mx(
-                    out=bank[:, 0 : span.stop - span.start],
-                    lhsT=codes[8 + i][:, g * P : (g + 1) * P].bitcast(FP8X4),
-                    lhsT_scale=scales[8 + i][:, g * P : (g + 1) * P],
-                    rhs=h_codes[g][:, span].bitcast(FP8X4),
-                    rhs_scale=h_scales[g][:, span],
-                    start=(g == 0),
-                    stop=(g == GROUPS - 1),
-                )
 
-        def lift_and_store(i, span, where):
+        def piece_of(i, n):
+            return half(n) if i == ROW_TILES - 1 else slice(0, F)
+
+        def cepstrum(i, n, g):
+            span = piece_of(i, n)
+            if g == 0:
+                take_bank(("sums", i, n))
+            nc.tensor.matmul_mx(
+                out=bank_of(("sums", i, n))[:, 0 : span.stop - span.start],
+                lhsT=codes[POWER_SOURCES + i][:, chunk(g)].bitcast(FP8X4),
+                lhsT_scale=scales[POWER_SOURCES + i][:, chunk(g)],
+                rhs=h_codes[g][:, span].bitcast(FP8X4),
+                rhs_scale=h_scales[g][:, span],
+                start=(g == 0),
+                stop=(g == GROUPS - 1),
+            )
+
+        def store(i, n, engine):
+            span = piece_of(i, n)
             width = span.stop - span.start
-            bank = last_read(("sums", i, span.start))[:, 0:width]
-            result = ring.tile([P, width], F32, name="result", tag="result", bufs=4)
-            if where == "V":
+            sums = bank_of(("sums", i, n))[:, 0:width]
+            result = ring.tile([P, width], F32, name="result", tag="result", bufs=RESULT_BUFS)
+            if engine == "V":
                 nc.vector.tensor_scalar(
-                    out=result[:], in0=bank, scalar1=cols[:, 16 + i : 17 + i], scalar2=None, op0=ALU.mult
+                    out=result[:], in0=sums, scalar1=vector_column(LIFTER_AT, i), scalar2=None, op0=ALU.mult
                 )
             else:
-                nc.scalar.activation(out=result[:], in_=bank, func=ACT.Copy, scale=cols[:, 16 + i : 17 + i])
-            nc.sync.dma_start(out=out[i * P : (i + 1) * P, span], in_=result[:])
+                nc.scalar.activation(out=result[:], in_=sums, func=ACT.Copy, scale=vector_column(LIFTER_AT, i))
+            give_back(("sums", i, n))
+            nc.sync.dma_start(out=out[chunk(i), span], in_=result[:])
 
-        def piece(i, n):
-            return slice(0, F) if i < QTILES - 1 else slice(256 * n, 256 * (n + 1))
+        steps = {
+            "load_source": load_source,
+            "load_filters": load_filters,
+            "load_weight": load_weight,
+            "load_vectors": load_vectors,
+            "widen_vectors": widen_vectors,
+            "turn_vectors": turn_vectors,
+            "keep_vectors": keep_vectors,
+            "sort_words": sort_words,
+            "turn_source": turn_source,
+            "pack": pack,
+            "quantize": quantize,
+            "pack_filters": pack_filters,
+            "quantize_filters": quantize_filters,
+            "mel": mel,
+            "log": log,
+            "level": level,
+            "turn_levels": turn_levels,
+            "weigh": weigh,
+            "quantize_h": quantize_h,
+            "cepstrum": cepstrum,
+            "store": store,
+        }
 
-        for token in ORDER.split():
-            name, where = token.split(":")
-            kind = name[0]
-            if name == "cast":
-                copier(where)(out=rows32[:], in_=rows16[:])
-                continue
-            if name == "tv":
-                nc.tensor.transpose(take_bank("vectors")[:, 0:P], rows32[:], ident[:])
-                continue
-            if name == "cols":
-                copier(where)(out=cols[:], in_=last_read("vectors")[:, 0:32])
-                continue
-            n = list(map(int, name[1:].split("_")))
-            if kind == "s":
-                sort_words(n[0], where)
-            elif kind == "t":
-                turn_operand(n[0], n[1])
-            elif kind == "c":
-                gather_operand(n[0], n[1], where)
-            elif kind == "q":
-                quantize_operand(n[0])
-            elif kind == "i":
-                interleave_filters(n[0], n[1], where)
-            elif kind == "f":
-                quantize_filters(n[0], n[1])
-            elif kind == "m":
-                mel_matmul(n[0], n[1], [n[2]])
-            elif kind == "l":
-                take_log(n[0], n[1])
-            elif kind == "a":
-                gain_and_bias(n[0], n[1], where)
-            elif kind == "u":
-                turn_levels(n[0], n[1])
-            elif kind == "h":
-                weigh_frames(n[0], n[1])
-            elif kind == "H":
-                quantize_h(n[0])
-            elif kind == "x":
-                cepstrum_matmul(n[0], piece(n[0], n[1]), [n[2]])
-            else:
-                lift_and_store(n[0], piece(n[0], n[1]), where)
+        make_identity(nc, ident[:])
+        nc.vector.memset(vector_rows16[:], 1.0)
+        nc.scalar.activation(out=vector_rows16[:], in_=vector_rows16[:], func=ACT.Ln)
+
+        for step in (LOADS + SCHEDULE).split():
+            fields = step.split(":")
+            steps[fields[0]](*[field if field in ("V", "S", "G") else int(field) for field in fields[1:]])

from contextlib import ExitStack

import concourse.mybir as mybir
from concourse.masks import make_identity

T, K, F, Q = 2048, 1024, 512, 1024
FLOPS = 2 * T * K * F + 2 * Q * T * F

F32 = mybir.dt.float32
BF16 = mybir.dt.bfloat16
U32 = mybir.dt.uint32
U8 = mybir.dt.uint8
FP8X4 = mybir.dt.float8_e4m3fn_x4
ACT = mybir.ActivationFunctionType
ALU = mybir.AluOpType

P = 128
PACK = 4
PASS = P * PACK
PASS_WORDS = PASS // 2
BANK = 512
BANKS = 8
GROUPS = T // PASS
BIN_PASSES = K // PASS
ROW_TILES = Q // P
HALF = F // 2

POWER_SOURCES = 2 * GROUPS
SOURCES = POWER_SOURCES + ROW_TILES

OFFSET_AT, GAIN_AT, BIAS_AT, LIFTER_AT, VECTOR_COLUMNS = 0, 4, 8, 16, 32

SORTED_BUFS, PACKED_BUFS, LOG_BUFS, LEVEL_BUFS, RESULT_BUFS = 4, 4, 4, 6, 4

LOADS = """
load_filters:0 load_source:0 load_vectors load_source:1 load_source:2 load_source:3 load_filters:1 load_weight
load_source:4 load_source:5 load_source:6 load_source:7 load_source:8 load_source:9 load_source:10
load_source:11 load_source:12 load_source:13 load_source:14 load_source:15
"""

SCHEDULE = """
pack_filters:0:0:V quantize_filters:0:0 pack_filters:0:1:V turn_source:0:0 turn_source:0:1 turn_source:1:0
    pack:0:0:S pack:0:1:V quantize_filters:0:1 pack:1:0:S turn_source:1:1 pack:1:1:S turn_source:2:0
    turn_source:2:1 widen_vectors quantize:0 turn_vectors turn_source:3:0 quantize:1 pack_filters:1:0:V
    pack:2:0:S pack:2:1:S pack:3:0:S pack_filters:1:1:S
mel:0:0:0 quantize_filters:1:0
turn_source:3:1 keep_vectors:S quantize:2
mel:0:1:0 mel:0:2:0 mel:0:0:1 quantize_filters:1:1 mel:0:3:0 pack:3:1:S log:0:0 sort_words:4:V mel:0:1:1
    mel:1:0:0 mel:0:2:1 sort_words:5:V mel:0:3:1
turn_source:4:0 log:0:1 level:0:0:S quantize:3 sort_words:6:V turn_source:4:1 turn_source:5:0 level:0:1:G
    turn_source:5:1 log:0:2 turn_levels:0:0 turn_source:6:0 log:0:3 pack:4:0:S pack:4:1:V pack:5:0:V
    sort_words:7:S pack:5:1:V pack:6:0:V
mel:1:0:1 mel:1:1:0 mel:1:1:1 log:1:0 log:1:1 mel:1:2:0 quantize:4 mel:1:2:1 mel:1:3:0 level:0:2:G mel:1:3:1
turn_levels:0:1 log:1:2 turn_source:6:1 level:0:3:G quantize:5 turn_source:7:0 log:1:3 sort_words:9:V
    turn_levels:0:2 weigh:0:0 pack:6:1:V turn_source:7:1 weigh:0:1 pack:7:0:S level:1:0:G turn_source:8:0
    level:1:1:S turn_source:8:1 pack:7:1:S
mel:2:0:0 mel:2:0:1 pack:8:0:S mel:2:1:0 mel:2:2:0 weigh:0:2 level:1:2:G quantize:6 mel:2:3:0 mel:2:1:1 log:2:0
    sort_words:10:V mel:2:2:1 quantize:7 mel:2:3:1 mel:3:0:0 mel:3:0:1 sort_words:11:V
turn_levels:0:3 pack:8:1:S turn_source:9:0 log:2:1 sort_words:12:V quantize:8 turn_levels:1:0 log:2:2
    level:1:3:G turn_levels:1:1 weigh:0:3 turn_source:9:1 turn_levels:1:2 log:2:3 level:2:0:G weigh:1:0
    turn_source:10:0 turn_source:10:1 weigh:1:1 turn_levels:1:3 level:2:1:G pack:9:0:S pack:9:1:S
mel:3:1:0 sort_words:13:S weigh:1:2 weigh:1:3 pack:10:0:S sort_words:14:V quantize_h:0 mel:3:2:0 mel:3:1:1
    pack:10:1:S mel:3:3:0 level:2:2:G mel:3:2:1 mel:3:3:1
turn_levels:2:0 log:3:0 turn_levels:2:1 level:2:3:G log:3:1 turn_levels:2:2 turn_source:11:0 quantize:9
    weigh:2:0 turn_levels:2:3 weigh:2:1 turn_source:11:1 level:3:0:G turn_levels:3:0 level:3:1:G
    turn_source:12:0 log:3:2 turn_source:12:1 weigh:2:2 turn_levels:3:1 log:3:3 pack:11:0:S level:3:2:G
    turn_levels:3:2 weigh:2:3 pack:11:1:S weigh:3:0 sort_words:15:S weigh:3:1 weigh:3:2 turn_source:13:0
    turn_source:13:1 turn_source:14:0 level:3:3:G pack:12:0:S quantize_h:1 turn_source:14:1 turn_source:15:0
    turn_source:15:1 quantize_h:2 turn_levels:3:3 pack:12:1:S
cepstrum:0:0:0 quantize:10 cepstrum:0:0:1 pack:13:0:S weigh:3:3 quantize:11 cepstrum:1:0:0 cepstrum:0:0:2
    cepstrum:1:0:1 pack:13:1:S cepstrum:1:0:2 cepstrum:2:0:0 cepstrum:2:0:1 quantize_h:3 cepstrum:3:0:0
    cepstrum:3:0:1 cepstrum:0:0:3 pack:14:0:S cepstrum:1:0:3 quantize:12 cepstrum:2:0:2 store:0:0:S quantize:13
    pack:14:1:S cepstrum:2:0:3 cepstrum:3:0:2 cepstrum:4:0:0 cepstrum:5:0:0 cepstrum:4:0:1 store:1:0:V
    cepstrum:3:0:3 store:2:0:V quantize:14 cepstrum:4:0:2 cepstrum:4:0:3 pack:15:0:S pack:15:1:V cepstrum:5:0:1
    cepstrum:6:0:0 store:3:0:S cepstrum:5:0:2 store:4:0:V quantize:15 cepstrum:5:0:3 cepstrum:6:0:1 store:5:0:S
    cepstrum:6:0:2 cepstrum:6:0:3 cepstrum:7:0:0 cepstrum:7:1:0 cepstrum:7:0:1 cepstrum:7:0:2 cepstrum:7:0:3
    store:6:0:V cepstrum:7:1:1 store:7:0:V cepstrum:7:1:2 cepstrum:7:1:3 store:7:1:V
"""


def tile_temporal_log_mel_cepstrum_f4_kernel(
    tc, power, filters, offset, gain, bias, frame_weight, basis, lifter, out
):
    nc = tc.nc
    copy_on = {"V": nc.vector.tensor_copy, "S": nc.scalar.copy}

    with ExitStack() as ctx:
        keep = ctx.enter_context(tc.tile_pool(name="keep", bufs=1))
        ring = ctx.enter_context(tc.tile_pool(name="ring", bufs=1))
        psum = ctx.enter_context(tc.psum_pool(name="psum", bufs=1))
        ctx.enter_context(tc.manual_schedule())

        idle_banks = ["bank%d" % n for n in range(BANKS)]
        held = {}

        def take_bank(use):
            tag = idle_banks[0]
            idle_banks.remove(tag)
            held[use] = (tag, psum.tile([P, BANK], F32, name=tag, tag=tag))

        def bank_of(use):
            return held[use][1]

        def give_back(use):
            idle_banks.append(held[use][0])

        ident = keep.tile([P, P], F32, name="ident")
        vector_rows16 = keep.tile([P, P], BF16, name="vector_rows16")
        vector_rows32 = keep.tile([P, P], F32, name="vector_rows32")
        vectors = keep.tile([P, VECTOR_COLUMNS], F32, name="vectors")
        weight = keep.tile([P, GROUPS, PACK], BF16, name="weight")

        def mx_tiles(name, count, width):
            code_tiles = [keep.tile([P, width], U32, name="%s_codes%d" % (name, n), align_bytes=64) for n in range(count)]
            scale_tiles = [keep.tile([P, width], U8, name="%s_scales%d" % (name, n), align_bytes=64) for n in range(count)]
            return code_tiles, scale_tiles

        source = [keep.tile([P, PACK, PASS], BF16, name="source%d" % a) for a in range(SOURCES)]
        codes, scales = mx_tiles("operand", SOURCES, PASS)
        filter_rows = [keep.tile([P, PACK, F], BF16, name="filter_rows%d" % c) for c in range(BIN_PASSES)]
        filter_16 = [keep.tile([P, F, PACK], BF16, name="filter_16_%d" % c, align_bytes=64) for c in range(BIN_PASSES)]
        filter_codes, filter_scales = mx_tiles("filter", BIN_PASSES, F)
        h_16 = [keep.tile([P, F, PACK], BF16, name="h_16_%d" % g, align_bytes=64) for g in range(GROUPS)]
        h_codes, h_scales = mx_tiles("h", GROUPS, F)

        def vector_column(first, n):
            return vectors[:, first + n : first + n + 1]

        def chunk(j):
            return slice(j * P, (j + 1) * P)

        def half(n):
            return slice(n * HALF, (n + 1) * HALF)


        def load_source(a):
            if a < POWER_SOURCES:
                g, r = divmod(a, 2)
                rows = power[g * PASS : (g + 1) * PASS, :].rearrange("(m t) (c k) -> m t c k", t=PACK, c=BIN_PASSES)
                src = rows[:, 2 * r : 2 * r + 2].rearrange("m t c k -> m (t c) k")
            else:
                src = basis[chunk(a - POWER_SOURCES), :].rearrange("q (g k) -> q g k", g=GROUPS)
            nc.sync.dma_start(out=source[a][:], in_=src)

        def load_filters(c):
            src = filters[c * PASS : (c + 1) * PASS, :].rearrange("(p t) f -> p t f", t=PACK)
            nc.sync.dma_start(out=filter_rows[c][:], in_=src)

        def load_weight():
            nc.sync.dma_start(out=weight[:], in_=frame_weight.rearrange("(g p t) -> p g t", p=P, t=PACK))

        def load_vectors():
            for vector, first in ((offset, OFFSET_AT), (gain, GAIN_AT), (bias, BIAS_AT), (lifter, LIFTER_AT)):
                rows = vector.rearrange("(j p) -> j p", p=P)
                nc.scalar.dma_start(out=vector_rows16[first : first + rows.shape[0], :], in_=rows)


        def widen_vectors():
            nc.vector.tensor_copy(out=vector_rows32[:], in_=vector_rows16[:])

        def turn_vectors():
            take_bank("vectors")
            nc.tensor.transpose(bank_of("vectors")[:, 0:P], vector_rows32[:], ident[:])

        def keep_vectors(engine):
            copy_on[engine](out=vectors[:], in_=bank_of("vectors")[:, 0:VECTOR_COLUMNS])
            give_back("vectors")


        sorted_words = {}
        packed = {}

        def words_of(a):
            return source[a][:].rearrange("p s k -> p (s k)").bitcast(F32)

        def sort_words(a, engine):
            sorted_words[a] = ring.tile([P, PACK, 2, P], F32, name="sorted", tag="sorted", bufs=SORTED_BUFS)
            copy_on[engine](out=sorted_words[a][:], in_=words_of(a).rearrange("p (s w u) -> p s u w", s=PACK, u=2))

        def turn_source(a, b):
            take_bank(("source", a, b))
            view = bank_of(("source", a, b))[:].rearrange("p (n u m) -> p n u m", n=2, u=2)
            for n in range(2):
                s = 2 * n + b if a < POWER_SOURCES else 2 * b + n
                for u in range(2):
                    if a in sorted_words:
                        piece = sorted_words[a][:, s, u, :]
                    else:
                        piece = words_of(a)[:, PASS_WORDS * s + u : PASS_WORDS * (s + 1) : 2]
                    nc.tensor.transpose(view[:, n, u, :], piece, ident[:])

        def pack(a, b, engine):
            if a < POWER_SOURCES:
                g, part = divmod(a, 2)
                operand = BIN_PASSES * g + b
            else:
                operand, part = a, b
            if operand not in packed:
                packed[operand] = ring.tile(
                    [P, PASS * PACK], BF16, name="packed", tag="packed", bufs=PACKED_BUFS, align_bytes=64
                )
            dst = packed[operand][:].bitcast(F32)[:, BANK * part : BANK * (part + 1)]
            copy_on[engine](
                out=dst.rearrange("p (n m u) -> p n m u", n=2, u=2),
                in_=bank_of(("source", a, b))[:].rearrange("p (n u m) -> p n m u", n=2, u=2),
            )
            give_back(("source", a, b))

        def quantize(operand):
            nc.vector.quantize_mx(out=codes[operand][:].bitcast(FP8X4), scales=scales[operand][:], in_=packed[operand][:])


        def pack_filters(c, n, engine):
            copy_on[engine](
                out=filter_16[c][:, half(n), :].rearrange("p (f i) t -> p f t i", i=PACK),
                in_=filter_rows[c][:, :, half(n)].rearrange("p t (f i) -> p f t i", i=PACK),
            )

        def quantize_filters(c, n):
            nc.vector.quantize_mx(
                out=filter_codes[c][:, half(n)].bitcast(FP8X4),
                scales=filter_scales[c][:, half(n)],
                in_=filter_16[c][:, half(n), :].rearrange("p f t -> p (f t)"),
            )


        logs = {}
        levels = {}

        def mel(g, j, c):
            if c == 0:
                take_bank(("energy", g, j))
            operand = BIN_PASSES * g + c
            nc.tensor.matmul_mx(
                out=bank_of(("energy", g, j))[:],
                lhsT=filter_codes[c][:, chunk(j)].bitcast(FP8X4),
                lhsT_scale=filter_scales[c][:, chunk(j)],
                rhs=codes[operand][:].bitcast(FP8X4),
                rhs_scale=scales[operand][:],
                start=(c == 0),
                stop=(c == BIN_PASSES - 1),
            )

        def log(g, j):
            logs[g, j] = ring.tile([P, PASS], F32, name="logs", tag="logs", bufs=LOG_BUFS)
            nc.scalar.activation(
                out=logs[g, j][:], in_=bank_of(("energy", g, j))[:], func=ACT.Ln, bias=vector_column(OFFSET_AT, j)
            )
            give_back(("energy", g, j))

        def level(g, j, engine):
            levels[g, j] = ring.tile([P, PASS], F32, name="levels", tag="levels", bufs=LEVEL_BUFS)
            if engine == "S":
                nc.scalar.activation(
                    out=levels[g, j][:],
                    in_=logs[g, j][:],
                    func=ACT.Identity,
                    scale=vector_column(GAIN_AT, j),
                    bias=vector_column(BIAS_AT, j),
                )
            else:
                nc.gpsimd.tensor_scalar(
                    out=levels[g, j][:],
                    in0=logs[g, j][:],
                    scalar1=vector_column(GAIN_AT, j),
                    scalar2=vector_column(BIAS_AT, j),
                    op0=ALU.mult,
                    op1=ALU.add,
                )

        def turn_levels(g, j):
            take_bank(("levels", g, j))
            for t in range(PACK):
                nc.tensor.transpose(bank_of(("levels", g, j))[:, chunk(t)], levels[g, j][:, chunk(t)], ident[:])

        def weigh(g, j):
            nc.vector.tensor_tensor(
                out=h_16[g][:, chunk(j), :],
                in0=bank_of(("levels", g, j))[:].rearrange("p (t f) -> p f t", t=PACK),
                in1=weight[:, g, :].unsqueeze(1).broadcast_to([P, P, PACK]),
                op=ALU.mult,
            )
            give_back(("levels", g, j))

        def quantize_h(g):
            nc.vector.quantize_mx(
                out=h_codes[g][:].bitcast(FP8X4), scales=h_scales[g][:], in_=h_16[g][:].rearrange("p f t -> p (f t)")
            )


        def piece_of(i, n):
            return half(n) if i == ROW_TILES - 1 else slice(0, F)

        def cepstrum(i, n, g):
            span = piece_of(i, n)
            if g == 0:
                take_bank(("sums", i, n))
            nc.tensor.matmul_mx(
                out=bank_of(("sums", i, n))[:, 0 : span.stop - span.start],
                lhsT=codes[POWER_SOURCES + i][:, chunk(g)].bitcast(FP8X4),
                lhsT_scale=scales[POWER_SOURCES + i][:, chunk(g)],
                rhs=h_codes[g][:, span].bitcast(FP8X4),
                rhs_scale=h_scales[g][:, span],
                start=(g == 0),
                stop=(g == GROUPS - 1),
            )

        def store(i, n, engine):
            span = piece_of(i, n)
            width = span.stop - span.start
            sums = bank_of(("sums", i, n))[:, 0:width]
            result = ring.tile([P, width], F32, name="result", tag="result", bufs=RESULT_BUFS)
            if engine == "V":
                nc.vector.tensor_scalar(
                    out=result[:], in0=sums, scalar1=vector_column(LIFTER_AT, i), scalar2=None, op0=ALU.mult
                )
            else:
                nc.scalar.activation(out=result[:], in_=sums, func=ACT.Copy, scale=vector_column(LIFTER_AT, i))
            give_back(("sums", i, n))
            nc.sync.dma_start(out=out[chunk(i), span], in_=result[:])

        steps = {
            "load_source": load_source,
            "load_filters": load_filters,
            "load_weight": load_weight,
            "load_vectors": load_vectors,
            "widen_vectors": widen_vectors,
            "turn_vectors": turn_vectors,
            "keep_vectors": keep_vectors,
            "sort_words": sort_words,
            "turn_source": turn_source,
            "pack": pack,
            "quantize": quantize,
            "pack_filters": pack_filters,
            "quantize_filters": quantize_filters,
            "mel": mel,
            "log": log,
            "level": level,
            "turn_levels": turn_levels,
            "weigh": weigh,
            "quantize_h": quantize_h,
            "cepstrum": cepstrum,
            "store": store,
        }

        make_identity(nc, ident[:])
        nc.vector.memset(vector_rows16[:], 1.0)
        nc.scalar.activation(out=vector_rows16[:], in_=vector_rows16[:], func=ACT.Ln)

        for step in (LOADS + SCHEDULE).split():
            fields = step.split(":")
            steps[fields[0]](*[field if field in ("V", "S", "G") else int(field) for field in fields[1:]])
